import numpy as np
import ml_dtypes


def mxq(x, axis, fmt="e4m3"):
    dtype, down = {"e4m3": (ml_dtypes.float8_e4m3fn, 7), "e5m2": (ml_dtypes.float8_e5m2, 14)}[fmt]
    v = np.moveaxis(np.asarray(x, np.float32).astype(ml_dtypes.bfloat16).astype(np.float64), axis, -1)
    blocks = v.reshape(v.shape[:-1] + (-1, 32))
    amax = np.abs(blocks).max(-1, keepdims=True)
    byte = np.maximum(np.where(amax > 0, np.frexp(amax)[1] - 1 + 127, 0) - down, 1)
    scale = np.exp2(byte - 127.0)
    codes = (blocks / scale).astype(np.float32).astype(dtype).astype(np.float64)
    return np.moveaxis((codes * scale).reshape(v.shape), -1, axis)


WIDE = False


def mx_kscale(k):
    if not WIDE:
        return np.ones(k)
    levels = np.array([10, -10, 5, -5, 0])
    if k % 512:
        return np.exp2(np.random.permutation(np.resize(levels, k // 32))).repeat(32)
    a = np.empty((k // 512, 16))
    for p in range(k // 512):
        a[p, :8] = np.random.permutation(np.resize(levels, 8))
        for g in range(8):
            far = levels[np.abs(levels - a[p, g]) >= 10]
            a[p, g + 8] = far[np.random.randint(len(far))]
    return np.exp2(a.ravel()).repeat(32)


BF16 = ml_dtypes.bfloat16


def bf(x):
    return np.asarray(x, np.float32).astype(BF16)


def f64(x):
    return np.asarray(x).astype(np.float64)


E2M1 = np.array([0.0, 0.5, 1.0, 1.5, 2.0, 3.0, 4.0, 6.0, -0.0, -0.5, -1.0, -1.5, -2.0, -3.0, -4.0, -6.0])


def pack_weight(w, fmt):
    k, n = w.shape
    w = f64(bf(w)).reshape(k // 32, 32, n)
    amax = np.abs(w).max(1)
    if fmt == "e4m3":
        byte = np.frexp(amax)[1] - 1 + 127 - 7
    else:
        mant, ex = np.frexp(amax / 6.0)
        byte = np.where(mant > 0.5, ex, ex - 1) + 127
    byte = np.clip(np.where(amax > 0, byte, 1), 1, 254)
    scaled = (w * np.exp2(127.0 - byte)[:, None, :]).reshape(k, n).astype(np.float32)
    by_word = np.ascontiguousarray(scaled.reshape(k // 512, 128, 4, n).transpose(0, 1, 3, 2))
    if fmt == "e4m3":
        words = by_word.astype(ml_dtypes.float8_e4m3fn).view(np.uint8)
    else:
        c = by_word.astype(ml_dtypes.float4_e2m1fn).view(np.uint8) & 0xF
        words = c[..., 0::2] | (c[..., 1::2] << 4)
    return np.ascontiguousarray(words), np.ascontiguousarray(byte.astype(np.uint8).reshape(k // 512, 16, n))


def unpack_weight(words, scales, fmt):
    g, p, n, _ = words.shape
    if fmt == "e4m3":
        vals = np.ascontiguousarray(words).view(ml_dtypes.float8_e4m3fn).astype(np.float64)
    else:
        nib = np.empty((g, p, n, 4), np.uint8)
        nib[..., 0::2] = words & 0xF
        nib[..., 1::2] = words >> 4
        vals = E2M1[nib]
    vals = vals * np.repeat(np.exp2(scales.astype(np.float64) - 127.0), 8, axis=1)[..., None]
    return vals.transpose(0, 1, 3, 2).reshape(g * 512, n)
def pack4(w):
    words, scales = pack_weight(w, "e2m1")
    return words.reshape(words.shape[0], 128, -1), scales


def unpack4(words, scales):
    return unpack_weight(words.reshape(words.shape[0], 128, -1, 2), scales, "e2m1")


E4M3FN = np.array([(-1.0 if i & 128 else 1.0) * ((1.0 + (i & 7) / 8.0) * 2.0 ** (((i >> 3) & 15) - 7) if i & 120 else (i & 7) * 2.0 ** -9) for i in range(256)])


def e4m3fn_bytes(y):
    return np.clip(np.asarray(y, np.float64), -448.0, 448.0).astype(np.float32).astype(ml_dtypes.float8_e4m3fn).view(np.uint8)


def e4m3fn_values(b):
    return E4M3FN[b]


B, N, K, M, P = 512, 512, 4, 1024, 1024


def draw0():
    s, t = mx_kscale(N), mx_kscale(M)
    inputs = {
        "mask": bf(np.random.standard_normal((B, N)) * s),
        "hr": bf(np.random.standard_normal((K, N, M)) / np.sqrt(N) / s[:, None]),
        "hi": bf(np.random.standard_normal((K, N, M)) / np.sqrt(N) / s[:, None]),
        "omega": bf(np.random.uniform(0.2, 0.8, K) / K),
        "quench": bf(np.random.uniform(0.4, 0.8, M)),
        "rho": bf((1.0 + 0.2 * np.random.standard_normal(M)) * t),
    }
    words, scales = pack4(4.0 * np.random.standard_normal((M, P)) / np.sqrt(M) / t[:, None])
    inputs["bake_words"] = words
    inputs["bake_scales"] = scales
    return inputs


def aerial_image(mask, hr, hi, omega):
    mq = mxq(f64(mask), 1, "e4m3")
    er = mq @ mxq(f64(hr), 1, "e4m3")
    ei = mq @ mxq(f64(hi), 1, "e4m3")
    intensity = er * er + ei * ei
    return np.sum(f64(omega)[:, None, None] * intensity, axis=0)


def core(mask, hr, hi, omega, quench, rho, bake_words, bake_scales):
    aerial = aerial_image(mask, hr, hi, omega)
    acid = 1.0 - np.exp(-aerial)
    net = f64(rho)[None, :] * (acid - f64(quench)[None, :])
    z = mxq(net, 1, "e4m3") @ unpack4(bake_words, bake_scales)
    return 1.0 / (1.0 + np.exp(-z))


def setup_inputs():
    drawn = draw0()
    full = np.asarray(drawn['hr']).astype(np.float64)
    scale = (np.abs(full).reshape(4, 512, 8, 128).max(axis=(3,)) / 448.0).astype(np.float32)
    given = {}
    for key, value in drawn.items():
        if key == 'hr':
            given['hr_bytes'] = e4m3fn_bytes(full / np.repeat(scale.astype(np.float64), 128, axis=2))
            given['hr_scale'] = scale
        else:
            given[key] = value
    return given


def reference(mask, hr_bytes, hr_scale, hi, omega, quench, rho, bake_words, bake_scales):
    return core(mask, e4m3fn_values(hr_bytes) * np.repeat(hr_scale.astype(np.float64), 128, axis=2), hi, omega, quench, rho, bake_words, bake_scales)

@@ -1,0 +1,325 @@
+from contextlib import ExitStack
+
+import concourse.mybir as mybir
+from concourse.masks import make_identity
+
+B, N, K, M, P = 512, 512, 4, 1024, 1024
+FLOPS = 2 * (B * N * M * K * 2 + B * M * P)
+
+F32 = mybir.dt.float32
+BF16 = mybir.dt.bfloat16
+U8 = mybir.dt.uint8
+U32 = mybir.dt.uint32
+I32 = mybir.dt.int32
+FP8 = mybir.dt.float8_e4m3fn
+E4M3X4 = mybir.dt.float8_e4m3fn_x4
+E2M1X4 = mybir.dt.float4_e2m1fn_x4
+ALU = mybir.AluOpType
+ACT = mybir.ActivationFunctionType
+
+LANES = 128
+PACK = 4
+COLS = 512
+TILES = B // LANES
+HALVES = M // COLS
+BLOCKS = COLS // LANES
+SCALAR_COLS = (512, 0, 0, 0, 0, 0, 0, 0)
+
+
+def tile_socsaerialimageacidquencherbake_d1p_kernel(
+    tc, mask, hr_bytes, hr_scale, hi, omega, quench, rho, bake_words, bake_scales, out
+):
+    nc = tc.nc
+    with ExitStack() as ctx:
+        keep = ctx.enter_context(tc.tile_pool(name="keep", bufs=1))
+        work = ctx.enter_context(tc.tile_pool(name="work", bufs=3))
+        psum = ctx.enter_context(tc.psum_pool(name="psum", bufs=4))
+        ctx.enter_context(tc.manual_schedule())
+
+        sc = keep.tile([LANES, K, PACK, M // LANES], F32, name="sc")
+        nc.sync.dma_start(out=sc[:], in_=hr_scale.rearrange("a (p t) j -> p a t j", t=PACK))
+        om = keep.tile([LANES, K], BF16, name="om")
+        nc.scalar.dma_start(out=om[:], in_=omega.partition_broadcast(LANES))
+
+        hr_raw, hi_raw = {}, {}
+
+        def load_hr(n):
+            g, a = divmod(n, K)
+            t = keep.tile([LANES, PACK, COLS], U8, name="hrb%d" % n)
+            nc.sync.dma_start(
+                out=t[:],
+                in_=hr_bytes[a].rearrange("(p t) m -> p t m", t=PACK)[:, :, g * COLS : (g + 1) * COLS],
+            )
+            hr_raw[n] = t
+
+        def load_hi(n):
+            g, a = divmod(n, K)
+            t = keep.tile([LANES, PACK, COLS], BF16, name="hib%d" % n)
+            nc.sync.dma_start(
+                out=t[:],
+                in_=hi[a].rearrange("(p t) m -> p t m", t=PACK)[:, :, g * COLS : (g + 1) * COLS],
+            )
+            hi_raw[n] = t
+
+        load_hr(0)
+        mraw = keep.tile([LANES, TILES, N], BF16, name="mraw")
+        mview = mask.rearrange("(c p) n -> p c n", p=LANES)
+        nc.sync.dma_start(out=mraw[:, 0:2, :], in_=mview[:, 0:2, :])
+        nc.sync.dma_start(out=mraw[:, 2:4, :], in_=mview[:, 2:4, :])
+        load_hi(0)
+        rh = keep.tile([LANES, HALVES, PACK], BF16, name="rh")
+        nc.scalar.dma_start(out=rh[:], in_=rho.rearrange("(g p t) -> p g t", p=LANES, t=PACK))
+        qu = keep.tile([LANES, HALVES, PACK], BF16, name="qu")
+        nc.scalar.dma_start(out=qu[:], in_=quench.rearrange("(g p t) -> p g t", p=LANES, t=PACK))
+        for n in range(1, HALVES * K):
+            load_hr(n)
+            load_hi(n)
+            if n == 4:
+                bw = keep.tile([LANES, HALVES, 2 * P], U8, name="bw", align_bytes=64)
+                nc.sync.dma_start(out=bw[:].bitcast(I32), in_=bake_words.bitcast(I32).rearrange("g p w -> p g w"))
+        bs = keep.tile([LANES, HALVES, P], U8, name="bs", align_bytes=64)
+        nc.gpsimd.memset(bs[:].bitcast(I32), 0)
+        for q in range(4):
+            nc.sync.dma_start(
+                out=bs[32 * q : 32 * q + 4].bitcast(I32),
+                in_=bake_scales[:, 4 * q : 4 * q + 4, :].bitcast(I32).rearrange("g q w -> q g w"),
+            )
+
+        ident = keep.tile([LANES, LANES], F32, name="ident")
+        make_identity(nc, ident[:])
+        half = keep.tile([LANES, K], F32, name="half")
+        nc.gpsimd.memset(half[:], 0.5)
+        root = keep.tile([LANES, K], F32, name="root")
+        nc.gpsimd.tensor_tensor(out=root[:], in0=om[:], in1=half[:], op=ALU.pow)
+        nrho = keep.tile([LANES, HALVES, PACK], F32, name="nrho")
+        nc.gpsimd.tensor_scalar(out=nrho[:], in0=rh[:], scalar1=-1.0, scalar2=0.0, op0=ALU.mult, op1=ALU.add)
+        omq = keep.tile([LANES, HALVES, PACK], F32, name="omq")
+        nc.gpsimd.tensor_scalar(out=omq[:], in0=qu[:], scalar1=-1.0, scalar2=1.0, op0=ALU.mult, op1=ALU.add)
+
+        wide = {}
+
+        def widen(n, ts):
+            g, a = divmod(n, K)
+            if n not in wide:
+                wide[n] = work.tile([LANES, PACK, COLS], BF16, name="wide", tag="wide", bufs=2)
+            for t in ts:
+                for j in range(BLOCKS):
+                    cols = slice(j * LANES, (j + 1) * LANES)
+                    jj = g * BLOCKS + j
+                    nc.vector.tensor_scalar(
+                        out=wide[n][:, t, cols],
+                        in0=hr_raw[n][:, t, cols].bitcast(FP8),
+                        scalar1=sc[:, a, t, jj : jj + 1],
+                        scalar2=None,
+                        op0=ALU.mult,
+                    )
+
+        def group_tile():
+            return work.tile([LANES, COLS, PACK], BF16, name="grp", tag="grp", bufs=4, align_bytes=64)
+
+        def interleave(engine_copy, dst, src4, c0, c1):
+            d = dst[:, c0:c1, :].rearrange("p (c i) t -> p c t i", i=4)
+            s = src4[:, :, c0:c1].rearrange("p t (c i) -> p c t i", i=4)
+            engine_copy(out=d, in_=s)
+
+        def quantise(grp):
+            codes = work.tile([LANES, COLS], U32, name="codes", tag="codes", bufs=4, align_bytes=64)
+            scales = work.tile([LANES, COLS], U8, name="scales", tag="scales", bufs=4, align_bytes=64)
+            nc.vector.quantize_mx(
+                out=codes[:].bitcast(E4M3X4), scales=scales[:], in_=grp[:].rearrange("p c t -> p (c t)")
+            )
+            return codes, scales
+
+        widen(0, range(4))
+        g_hr = group_tile()
+        interleave(nc.vector.tensor_copy, g_hr, wide[0], 0, COLS)
+
+        mgrp = keep.tile([LANES, B, PACK], BF16, name="mgrp", align_bytes=64)
+        mwords = mraw[:].rearrange("p c n -> p (c n)").bitcast(F32)
+        for h in range(2):
+            bank = psum.tile([LANES, 2, 2, LANES], F32, name="mx", tag="mx", bufs=4)
+            for c in range(2):
+                for u in range(2):
+                    base = (2 * h + c) * (N // 2)
+                    nc.tensor.transpose(bank[:, c, u, :], mwords[:, base + u : base + N // 2 : 2], ident[:])
+            dst = mgrp[:, h * 256 : (h + 1) * 256, :].rearrange("p b t -> p (b t)").bitcast(F32)
+            nc.scalar.copy(
+                out=dst.rearrange("p (c r u) -> p c r u", c=2, u=2),
+                in_=bank[:].rearrange("p c u r -> p c r u"),
+            )
+        mcodes = keep.tile([LANES, B], U32, name="mcodes", align_bytes=64)
+        mscales = keep.tile([LANES, B], U8, name="mscales", align_bytes=64)
+
+        sq = {}
+        acc = {}
+
+        def multiply(u, codes, scales):
+            banks = []
+            for bt in range(TILES):
+                bank = psum.tile([LANES, COLS], F32, name="mx", tag="mx", bufs=4)
+                rows = slice(bt * LANES, (bt + 1) * LANES)
+                nc.tensor.matmul_mx(
+                    out=bank[:],
+                    lhsT=mcodes[:, rows].bitcast(E4M3X4),
+                    lhsT_scale=mscales[:, rows],
+                    rhs=codes[:].bitcast(E4M3X4),
+                    rhs_scale=scales[:],
+                    start=True,
+                    stop=True,
+                )
+                banks.append(bank)
+            return banks
+
+        def square(u, bt, bank):
+            a = (u // 2) % K
+            t = work.tile([LANES, PACK, LANES], F32, name="sq", tag="sq%d" % bt, bufs=3)
+            nc.scalar.activation(
+                out=t[:], in_=bank[:].rearrange("p (q t) -> p t q", t=PACK), func=ACT.Square, scale=root[:, a : a + 1]
+            )
+            sq[u, bt] = t
+
+        def turn(u, bt):
+            g, k = divmod(u, 2 * K)
+            if k == 0:
+                acc[g, bt] = psum.tile([LANES, PACK, LANES], F32, name="acc", tag="acc", bufs=4)
+            for t in range(PACK):
+                nc.tensor.matmul(
+                    acc[g, bt][:, t, :],
+                    lhsT=sq[u, bt][:, t, :],
+                    rhs=ident[:],
+                    is_transpose=True,
+                    start=(k == 0 and t == 0),
+                    stop=(k == 2 * K - 1 and t == PACK - 1),
+                )
+
+        def decay(g, bt, dst):
+            nc.scalar.activation(out=dst, in_=acc[g, bt][:], func=ACT.Exp, scale=-1.0)
+
+        e0 = keep.tile([LANES, TILES, PACK, LANES], F32, name="e0")
+        net0 = keep.tile([LANES, TILES, PACK, LANES], BF16, name="net0")
+        ngrp0 = keep.tile([LANES, TILES, LANES, PACK], BF16, name="ngrp0", align_bytes=64)
+        ncodes0 = keep.tile([LANES, B], U32, name="ncodes0", align_bytes=64)
+        nscales0 = keep.tile([LANES, B], U8, name="nscales0", align_bytes=64)
+
+        def hi_group(n):
+            grp = group_tile()
+            cut = SCALAR_COLS[n]
+            if cut:
+                interleave(nc.scalar.copy, grp, hi_raw[n], 0, cut)
+            if cut < COLS:
+                interleave(nc.vector.tensor_copy, grp, hi_raw[n], cut, COLS)
+            return grp
+
+        last = HALVES * K - 1
+        for n in range(HALVES * K):
+            if n > 0:
+                g_hr = group_tile()
+                interleave(nc.vector.tensor_copy, g_hr, wide[n], 0, COLS)
+            if n < last:
+                widen(n + 1, (0, 1))
+            if n == 0:
+                nc.vector.quantize_mx(
+                    out=mcodes[:].bitcast(E4M3X4), scales=mscales[:], in_=mgrp[:].rearrange("p b t -> p (b t)")
+                )
+            codes, scales = quantise(g_hr)
+            u = 2 * n
+            banks = multiply(u, codes, scales)
+            if n == 0:
+                g_hi = hi_group(n)
+            for bt in range(TILES):
+                square(u, bt, banks[bt])
+            if n == K:
+                for bt in range(TILES):
+                    turn(u - 1, bt)
+                for bt in range(TILES):
+                    decay(0, bt, e0[:, bt])
+            elif n > 0:
+                for bt in range(TILES):
+                    turn(u - 1, bt)
+            if n > 0:
+                g_hi = hi_group(n)
+            if n < last:
+                widen(n + 1, (2, 3))
+            if n == 6:
+                for t in range(PACK):
+                    nc.vector.tensor_scalar(
+                        out=net0[:, :, t, :],
+                        in0=e0[:, :, t, :],
+                        scalar1=omq[:, 0, t : t + 1],
+                        scalar2=nrho[:, 0, t : t + 1],
+                        op0=ALU.subtract,
+                        op1=ALU.mult,
+                    )
+            if n == 7:
+                nc.vector.tensor_copy(out=ngrp0[:], in_=net0[:].rearrange("p c t b -> p c b t"))
+            codes, scales = quantise(g_hi)
+            if n == 7:
+                nc.vector.quantize_mx(
+                    out=ncodes0[:].bitcast(E4M3X4),
+                    scales=nscales0[:],
+                    in_=ngrp0[:].rearrange("p c b t -> p (c b t)"),
+                )
+            banks = multiply(u + 1, codes, scales)
+            if n < last:
+                for bt in range(TILES):
+                    square(u + 1, bt, banks[bt])
+                for bt in range(TILES):
+                    turn(u, bt)
+
+        u = 2 * last + 1
+        e1 = {}
+
+        def finish_decay(bt):
+            e1[bt] = work.tile([LANES, PACK, LANES], F32, name="e1", tag="e1", bufs=4)
+            decay(1, bt, e1[bt][:])
+
+        for bt in range(TILES):
+            turn(u - 1, bt)
+        for bt in range(TILES):
+            square(u, bt, banks[bt])
+            turn(u, bt)
+            if bt >= 2:
+                finish_decay(bt - 2)
+        finish_decay(2)
+        finish_decay(3)
+
+        ncode1, nscale1 = {}, {}
+        for bt in range(TILES):
+            net1 = work.tile([LANES, PACK, LANES], BF16, name="net1", tag="net1", bufs=4)
+            for t in range(PACK):
+                nc.vector.tensor_scalar(
+                    out=net1[:, t, :],
+                    in0=e1[bt][:, t, :],
+                    scalar1=omq[:, 1, t : t + 1],
+                    scalar2=nrho[:, 1, t : t + 1],
+                    op0=ALU.subtract,
+                    op1=ALU.mult,
+                )
+            ngrp1 = work.tile([LANES, LANES, PACK], BF16, name="ngrp1", tag="ngrp1", bufs=4, align_bytes=64)
+            interleave(nc.vector.tensor_copy, ngrp1, net1, 0, LANES)
+            c1 = work.tile([LANES, LANES], U32, name="nc1", tag="nc1", bufs=4, align_bytes=64)
+            s1 = work.tile([LANES, LANES], U8, name="ns1", tag="ns1", bufs=4, align_bytes=64)
+            nc.vector.quantize_mx(
+                out=c1[:].bitcast(E4M3X4), scales=s1[:], in_=ngrp1[:].rearrange("p b t -> p (b t)")
+            )
+            ncode1[bt], nscale1[bt] = c1, s1
+
+        for bt in range(TILES):
+            rows = slice(bt * LANES, (bt + 1) * LANES)
+            for ph in range(2):
+                bank = psum.tile([LANES, COLS], F32, name="mx", tag="mx", bufs=4)
+                for g in range(HALVES):
+                    nc.tensor.matmul_mx(
+                        out=bank[:],
+                        lhsT=(ncodes0[:, rows] if g == 0 else ncode1[bt][:]).bitcast(E4M3X4),
+                        lhsT_scale=(nscales0[:, rows] if g == 0 else nscale1[bt][:]),
+                        rhs=bw[:, g, ph * 1024 : (ph + 1) * 1024].bitcast(E2M1X4),
+                        rhs_scale=bs[:, g, ph * COLS : (ph + 1) * COLS],
+                        start=(g == 0),
+                        stop=(g == HALVES - 1),
+                    )
+                th = work.tile([LANES, COLS], F32, name="th", tag="th", bufs=4)
+                nc.scalar.activation(out=th[:], in_=bank[:], func=ACT.Tanh, scale=0.5)
+                o = work.tile([LANES, COLS], F32, name="o", tag="o", bufs=4)
+                nc.vector.tensor_scalar(out=o[:], in0=th[:], scalar1=0.5, scalar2=0.5, op0=ALU.mult, op1=ALU.add)
+                nc.sync.dma_start(out=out[rows, ph * COLS : (ph + 1) * COLS], in_=o[:])

@@ -23,7 +23,10 @@ COLS = 512
 TILES = B // LANES
 HALVES = M // COLS
 BLOCKS = COLS // LANES
-SCALAR_COLS = (512, 0, 0, 0, 0, 0, 0, 0)
+PAIRS = HALVES * K
+SCALAR_COLS = (384, 192, 192, 192, 192, 192, 192, 192)
+PRE = ((), (), (), (), (), (), (), ())
+NET0 = (8, 8, 8)
 
 
 def tile_socsaerialimageacidquencherbake_d1p_kernel(
@@ -71,12 +74,11 @@ def tile_socsaerialimageacidquencherbake_d1p_kernel(
         nc.scalar.dma_start(out=rh[:], in_=rho.rearrange("(g p t) -> p g t", p=LANES, t=PACK))
         qu = keep.tile([LANES, HALVES, PACK], BF16, name="qu")
         nc.scalar.dma_start(out=qu[:], in_=quench.rearrange("(g p t) -> p g t", p=LANES, t=PACK))
-        for n in range(1, HALVES * K):
+        for n in range(1, PAIRS):
             load_hr(n)
             load_hi(n)
-            if n == 4:
-                bw = keep.tile([LANES, HALVES, 2 * P], U8, name="bw", align_bytes=64)
-                nc.sync.dma_start(out=bw[:].bitcast(I32), in_=bake_words.bitcast(I32).rearrange("g p w -> p g w"))
+        bw = keep.tile([LANES, HALVES, 2 * P], U8, name="bw", align_bytes=64)
+        nc.sync.dma_start(out=bw[:].bitcast(I32), in_=bake_words.bitcast(I32).rearrange("g p w -> p g w"))
         bs = keep.tile([LANES, HALVES, P], U8, name="bs", align_bytes=64)
         nc.gpsimd.memset(bs[:].bitcast(I32), 0)
         for q in range(4):
@@ -99,6 +101,8 @@ def tile_socsaerialimageacidquencherbake_d1p_kernel(
         wide = {}
 
         def widen(n, ts):
+            if n >= PAIRS:
+                return
             g, a = divmod(n, K)
             if n not in wide:
                 wide[n] = work.tile([LANES, PACK, COLS], BF16, name="wide", tag="wide", bufs=2)
@@ -115,7 +119,7 @@ def tile_socsaerialimageacidquencherbake_d1p_kernel(
                     )
 
         def group_tile():
-            return work.tile([LANES, COLS, PACK], BF16, name="grp", tag="grp", bufs=4, align_bytes=64)
+            return work.tile([LANES, COLS, PACK], BF16, name="grp", tag="grp", bufs=5, align_bytes=64)
 
         def interleave(engine_copy, dst, src4, c0, c1):
             d = dst[:, c0:c1, :].rearrange("p (c i) t -> p c t i", i=4)
@@ -129,6 +133,101 @@ def tile_socsaerialimageacidquencherbake_d1p_kernel(
                 out=codes[:].bitcast(E4M3X4), scales=scales[:], in_=grp[:].rearrange("p c t -> p (c t)")
             )
             return codes, scales
+
+        sq = {}
+        acc = {}
+
+        def multiply(codes, scales):
+            banks = []
+            for bt in range(TILES):
+                bank = psum.tile([LANES, COLS], F32, name="mx", tag="mx", bufs=4)
+                rows = slice(bt * LANES, (bt + 1) * LANES)
+                nc.tensor.matmul_mx(
+                    out=bank[:],
+                    lhsT=mcodes[:, rows].bitcast(E4M3X4),
+                    lhsT_scale=mscales[:, rows],
+                    rhs=codes[:].bitcast(E4M3X4),
+                    rhs_scale=scales[:],
+                    start=True,
+                    stop=True,
+                )
+                banks.append(bank)
+            return banks
+
+        def square(u, bt, bank):
+            a = (u // 2) % K
+            t = work.tile([LANES, PACK, LANES], F32, name="sq", tag="sq%d" % bt, bufs=4)
+            nc.scalar.activation(
+                out=t[:], in_=bank[:].rearrange("p (q t) -> p t q", t=PACK), func=ACT.Square, scale=root[:, a : a + 1]
+            )
+            sq[u, bt] = t
+
+        def preadd(n, bt):
+            s = work.tile([LANES, PACK, LANES], F32, name="sum", tag="sum", bufs=4)
+            nc.vector.tensor_tensor(out=s[:], in0=sq[2 * n, bt][:], in1=sq[2 * n + 1, bt][:], op=ALU.add)
+            sq[2 * n + 1, bt] = s
+
+        def turn(u, bt):
+            n, odd = divmod(u, 2)
+            g, a = divmod(n, K)
+            if not odd and bt in PRE[n]:
+                return
+            first = (g, bt) not in acc
+            if first:
+                acc[g, bt] = psum.tile([LANES, PACK, LANES], F32, name="acc", tag="acc", bufs=4)
+            final = odd and a == K - 1
+            for t in range(PACK):
+                nc.tensor.matmul(
+                    acc[g, bt][:, t, :],
+                    lhsT=sq[u, bt][:, t, :],
+                    rhs=ident[:],
+                    is_transpose=True,
+                    start=bool(first and t == 0),
+                    stop=bool(final and t == PACK - 1),
+                )
+
+        def decay(g, bt, dst):
+            nc.scalar.activation(out=dst, in_=acc[g, bt][:], func=ACT.Exp, scale=-1.0)
+
+        e0 = keep.tile([LANES, TILES, PACK, LANES], F32, name="e0")
+        net0 = keep.tile([LANES, TILES, PACK, LANES], BF16, name="net0")
+        ngrp0 = keep.tile([LANES, TILES, LANES, PACK], BF16, name="ngrp0", align_bytes=64)
+        ncodes0 = keep.tile([LANES, B], U32, name="ncodes0", align_bytes=64)
+        nscales0 = keep.tile([LANES, B], U8, name="nscales0", align_bytes=64)
+
+        hi_grp = {}
+
+        def hi_vector(n):
+            cut = SCALAR_COLS[n]
+            if n not in hi_grp:
+                hi_grp[n] = group_tile()
+            if cut < COLS:
+                interleave(nc.vector.tensor_copy, hi_grp[n], hi_raw[n], cut, COLS)
+
+        def hi_scalar(n):
+            if n < PAIRS and SCALAR_COLS[n]:
+                hi_grp[n] = group_tile()
+                interleave(nc.scalar.copy, hi_grp[n], hi_raw[n], 0, SCALAR_COLS[n])
+
+        def net0_step(n):
+            if n == NET0[0]:
+                for t in range(PACK):
+                    nc.vector.tensor_scalar(
+                        out=net0[:, :, t, :],
+                        in0=e0[:, :, t, :],
+                        scalar1=omq[:, 0, t : t + 1],
+                        scalar2=nrho[:, 0, t : t + 1],
+                        op0=ALU.subtract,
+                        op1=ALU.mult,
+                    )
+            if n == NET0[1]:
+                nc.vector.tensor_copy(out=ngrp0[:], in_=net0[:].rearrange("p c t b -> p c b t"))
+            if n == NET0[2]:
+                nc.vector.quantize_mx(
+                    out=ncodes0[:].bitcast(E4M3X4),
+                    scales=nscales0[:],
+                    in_=ngrp0[:].rearrange("p c b t -> p (c b t)"),
+                )
 
         widen(0, range(4))
         g_hr = group_tile()
@@ -149,124 +248,51 @@ def tile_socsaerialimageacidquencherbake_d1p_kernel(
             )
         mcodes = keep.tile([LANES, B], U32, name="mcodes", align_bytes=64)
         mscales = keep.tile([LANES, B], U8, name="mscales", align_bytes=64)
+        nc.vector.quantize_mx(
+            out=mcodes[:].bitcast(E4M3X4), scales=mscales[:], in_=mgrp[:].rearrange("p b t -> p (b t)")
+        )
 
-        sq = {}
-        acc = {}
-
-        def multiply(u, codes, scales):
-            banks = []
-            for bt in range(TILES):
-                bank = psum.tile([LANES, COLS], F32, name="mx", tag="mx", bufs=4)
-                rows = slice(bt * LANES, (bt + 1) * LANES)
-                nc.tensor.matmul_mx(
-                    out=bank[:],
-                    lhsT=mcodes[:, rows].bitcast(E4M3X4),
-                    lhsT_scale=mscales[:, rows],
-                    rhs=codes[:].bitcast(E4M3X4),
-                    rhs_scale=scales[:],
-                    start=True,
-                    stop=True,
-                )
-                banks.append(bank)
-            return banks
-
-        def square(u, bt, bank):
-            a = (u // 2) % K
-            t = work.tile([LANES, PACK, LANES], F32, name="sq", tag="sq%d" % bt, bufs=3)
-            nc.scalar.activation(
-                out=t[:], in_=bank[:].rearrange("p (q t) -> p t q", t=PACK), func=ACT.Square, scale=root[:, a : a + 1]
-            )
-            sq[u, bt] = t
-
-        def turn(u, bt):
-            g, k = divmod(u, 2 * K)
-            if k == 0:
-                acc[g, bt] = psum.tile([LANES, PACK, LANES], F32, name="acc", tag="acc", bufs=4)
-            for t in range(PACK):
-                nc.tensor.matmul(
-                    acc[g, bt][:, t, :],
-                    lhsT=sq[u, bt][:, t, :],
-                    rhs=ident[:],
-                    is_transpose=True,
-                    start=(k == 0 and t == 0),
-                    stop=(k == 2 * K - 1 and t == PACK - 1),
-                )
-
-        def decay(g, bt, dst):
-            nc.scalar.activation(out=dst, in_=acc[g, bt][:], func=ACT.Exp, scale=-1.0)
-
-        e0 = keep.tile([LANES, TILES, PACK, LANES], F32, name="e0")
-        net0 = keep.tile([LANES, TILES, PACK, LANES], BF16, name="net0")
-        ngrp0 = keep.tile([LANES, TILES, LANES, PACK], BF16, name="ngrp0", align_bytes=64)
-        ncodes0 = keep.tile([LANES, B], U32, name="ncodes0", align_bytes=64)
-        nscales0 = keep.tile([LANES, B], U8, name="nscales0", align_bytes=64)
-
-        def hi_group(n):
-            grp = group_tile()
-            cut = SCALAR_COLS[n]
-            if cut:
-                interleave(nc.scalar.copy, grp, hi_raw[n], 0, cut)
-            if cut < COLS:
-                interleave(nc.vector.tensor_copy, grp, hi_raw[n], cut, COLS)
-            return grp
-
-        last = HALVES * K - 1
-        for n in range(HALVES * K):
+        for n in range(PAIRS):
+            u = 2 * n
             if n > 0:
                 g_hr = group_tile()
                 interleave(nc.vector.tensor_copy, g_hr, wide[n], 0, COLS)
-            if n < last:
                 widen(n + 1, (0, 1))
-            if n == 0:
-                nc.vector.quantize_mx(
-                    out=mcodes[:].bitcast(E4M3X4), scales=mscales[:], in_=mgrp[:].rearrange("p b t -> p (b t)")
-                )
             codes, scales = quantise(g_hr)
-            u = 2 * n
-            banks = multiply(u, codes, scales)
+            banks = multiply(codes, scales)
             if n == 0:
-                g_hi = hi_group(n)
+                hi_scalar(0)
             for bt in range(TILES):
                 square(u, bt, banks[bt])
-            if n == K:
-                for bt in range(TILES):
-                    turn(u - 1, bt)
-                for bt in range(TILES):
-                    decay(0, bt, e0[:, bt])
-            elif n > 0:
-                for bt in range(TILES):
-                    turn(u - 1, bt)
+            hi_scalar(n + 1)
             if n > 0:
-                g_hi = hi_group(n)
-            if n < last:
+                for bt in range(TILES):
+                    if bt not in PRE[n - 1]:
+                        turn(u - 1, bt)
+                if n == K:
+                    for bt in range(TILES):
+                        decay(0, bt, e0[:, bt])
+                hi_vector(n)
                 widen(n + 1, (2, 3))
-            if n == 6:
-                for t in range(PACK):
-                    nc.vector.tensor_scalar(
-                        out=net0[:, :, t, :],
-                        in0=e0[:, :, t, :],
-                        scalar1=omq[:, 0, t : t + 1],
-                        scalar2=nrho[:, 0, t : t + 1],
-                        op0=ALU.subtract,
-                        op1=ALU.mult,
-                    )
-            if n == 7:
-                nc.vector.tensor_copy(out=ngrp0[:], in_=net0[:].rearrange("p c t b -> p c b t"))
-            codes, scales = quantise(g_hi)
-            if n == 7:
-                nc.vector.quantize_mx(
-                    out=ncodes0[:].bitcast(E4M3X4),
-                    scales=nscales0[:],
-                    in_=ngrp0[:].rearrange("p c b t -> p (c b t)"),
-                )
-            banks = multiply(u + 1, codes, scales)
-            if n < last:
+                net0_step(n)
+            else:
+                hi_vector(n)
+                widen(n + 1, (0, 1))
+            codes, scales = quantise(hi_grp[n])
+            if n == 0:
+                widen(n + 1, (2, 3))
+            banks = multiply(codes, scales)
+            if n < PAIRS - 1:
                 for bt in range(TILES):
                     square(u + 1, bt, banks[bt])
                 for bt in range(TILES):
                     turn(u, bt)
 
-        u = 2 * last + 1
+        u = 2 * PAIRS - 1
+        net0_step(PAIRS)
+
+        for bt in range(TILES):
+            turn(u - 1, bt)
         e1 = {}
 
         def finish_decay(bt):
@@ -274,52 +300,77 @@ def tile_socsaerialimageacidquencherbake_d1p_kernel(
             decay(1, bt, e1[bt][:])
 
         for bt in range(TILES):
-            turn(u - 1, bt)
-        for bt in range(TILES):
             square(u, bt, banks[bt])
+            if bt in PRE[PAIRS - 1]:
+                preadd(PAIRS - 1, bt)
             turn(u, bt)
             if bt >= 2:
                 finish_decay(bt - 2)
         finish_decay(2)
         finish_decay(3)
 
-        ncode1, nscale1 = {}, {}
-        for bt in range(TILES):
-            net1 = work.tile([LANES, PACK, LANES], BF16, name="net1", tag="net1", bufs=4)
+        net1, ngrp1, ncode1, nscale1 = {}, {}, {}, {}
+
+        def net_affine(bt):
+            net1[bt] = work.tile([LANES, PACK, LANES], BF16, name="net1", tag="net1", bufs=4)
             for t in range(PACK):
                 nc.vector.tensor_scalar(
-                    out=net1[:, t, :],
+                    out=net1[bt][:, t, :],
                     in0=e1[bt][:, t, :],
                     scalar1=omq[:, 1, t : t + 1],
                     scalar2=nrho[:, 1, t : t + 1],
                     op0=ALU.subtract,
                     op1=ALU.mult,
                 )
-            ngrp1 = work.tile([LANES, LANES, PACK], BF16, name="ngrp1", tag="ngrp1", bufs=4, align_bytes=64)
-            interleave(nc.vector.tensor_copy, ngrp1, net1, 0, LANES)
+
+        def net_group(bt):
+            ngrp1[bt] = work.tile([LANES, LANES, PACK], BF16, name="ngrp1", tag="ngrp1", bufs=4, align_bytes=64)
+            interleave(nc.vector.tensor_copy, ngrp1[bt], net1[bt], 0, LANES)
+
+        def net_quantise(bt):
             c1 = work.tile([LANES, LANES], U32, name="nc1", tag="nc1", bufs=4, align_bytes=64)
             s1 = work.tile([LANES, LANES], U8, name="ns1", tag="ns1", bufs=4, align_bytes=64)
             nc.vector.quantize_mx(
-                out=c1[:].bitcast(E4M3X4), scales=s1[:], in_=ngrp1[:].rearrange("p b t -> p (b t)")
+                out=c1[:].bitcast(E4M3X4), scales=s1[:], in_=ngrp1[bt][:].rearrange("p b t -> p (b t)")
             )
             ncode1[bt], nscale1[bt] = c1, s1
 
+        net_affine(0)
         for bt in range(TILES):
+            net_group(bt)
+            if bt + 1 < TILES:
+                net_affine(bt + 1)
+            net_quantise(bt)
+
+        z = {}
+
+        def bake(g, bt, ph):
+            if g == 0:
+                z[bt, ph] = psum.tile([LANES, COLS], F32, name="z", tag=("mx" if bt < 2 else "acc"), bufs=4)
             rows = slice(bt * LANES, (bt + 1) * LANES)
-            for ph in range(2):
-                bank = psum.tile([LANES, COLS], F32, name="mx", tag="mx", bufs=4)
-                for g in range(HALVES):
-                    nc.tensor.matmul_mx(
-                        out=bank[:],
-                        lhsT=(ncodes0[:, rows] if g == 0 else ncode1[bt][:]).bitcast(E4M3X4),
-                        lhsT_scale=(nscales0[:, rows] if g == 0 else nscale1[bt][:]),
-                        rhs=bw[:, g, ph * 1024 : (ph + 1) * 1024].bitcast(E2M1X4),
-                        rhs_scale=bs[:, g, ph * COLS : (ph + 1) * COLS],
-                        start=(g == 0),
-                        stop=(g == HALVES - 1),
-                    )
-                th = work.tile([LANES, COLS], F32, name="th", tag="th", bufs=4)
-                nc.scalar.activation(out=th[:], in_=bank[:], func=ACT.Tanh, scale=0.5)
-                o = work.tile([LANES, COLS], F32, name="o", tag="o", bufs=4)
-                nc.vector.tensor_scalar(out=o[:], in0=th[:], scalar1=0.5, scalar2=0.5, op0=ALU.mult, op1=ALU.add)
-                nc.sync.dma_start(out=out[rows, ph * COLS : (ph + 1) * COLS], in_=o[:])
+            nc.tensor.matmul_mx(
+                out=z[bt, ph][:],
+                lhsT=(ncodes0[:, rows] if g == 0 else ncode1[bt][:]).bitcast(E4M3X4),
+                lhsT_scale=(nscales0[:, rows] if g == 0 else nscale1[bt][:]),
+                rhs=bw[:, g, ph * 1024 : (ph + 1) * 1024].bitcast(E2M1X4),
+                rhs_scale=bs[:, g, ph * COLS : (ph + 1) * COLS],
+                start=(g == 0),
+                stop=(g == HALVES - 1),
+            )
+
+        def finish(bt, ph):
+            rows = slice(bt * LANES, (bt + 1) * LANES)
+            th = work.tile([LANES, COLS], F32, name="th", tag="th", bufs=4)
+            nc.scalar.activation(out=th[:], in_=z[bt, ph][:], func=ACT.Tanh, scale=0.5)
+            o = work.tile([LANES, COLS], F32, name="o", tag="o", bufs=8)
+            nc.vector.tensor_scalar(out=o[:], in0=th[:], scalar1=0.5, scalar2=0.5, op0=ALU.mult, op1=ALU.add)
+            nc.sync.dma_start(out=out[rows, ph * COLS : (ph + 1) * COLS], in_=o[:])
+
+        for h in range(2):
+            for bt in (2 * h, 2 * h + 1):
+                for ph in range(2):
+                    bake(0, bt, ph)
+            for bt in (2 * h, 2 * h + 1):
+                for ph in range(2):
+                    bake(1, bt, ph)
+                    finish(bt, ph)

@@ -24,9 +24,13 @@ TILES = B // LANES
 HALVES = M // COLS
 BLOCKS = COLS // LANES
 PAIRS = HALVES * K
-SCALAR_COLS = (384, 192, 192, 192, 192, 192, 192, 192)
-PRE = ((), (), (), (), (), (), (), ())
+SCALAR_COLS = (256, 0, 0, 0, 0, 0, 0, 0)
+PRE = ((), (), (), (), (), (), (), (0, 1, 2, 3,))
 NET0 = (8, 8, 8)
+RUN = 4
+WARM = (6, 6)
+WIDEN_A = (5, 0, 0, 0, 0, 0, 0, 0)
+WIDEN_B = (0, 0, 0, 0, 0, 0, 0, 0)
 
 
 def tile_socsaerialimageacidquencherbake_d1p_kernel(
@@ -100,23 +104,34 @@ def tile_socsaerialimageacidquencherbake_d1p_kernel(
 
         wide = {}
 
+        def widen_block(engine, n, t, j):
+            g, a = divmod(n, K)
+            if n not in wide:
+                wide[n] = work.tile([LANES, PACK, COLS], BF16, name="wide", tag="wide", bufs=3)
+            cols = slice(j * LANES, (j + 1) * LANES)
+            scale = sc[:, a, t, g * BLOCKS + j : g * BLOCKS + j + 1]
+            dst = wide[n][:, t, cols]
+            src = hr_raw[n][:, t, cols].bitcast(FP8)
+            if engine == "S":
+                nc.scalar.activation(out=dst, in_=src, func=ACT.Copy, scale=scale)
+            else:
+                nc.vector.tensor_scalar(out=dst, in0=src, scalar1=scale, scalar2=None, op0=ALU.mult)
+
         def widen(n, ts):
             if n >= PAIRS:
                 return
-            g, a = divmod(n, K)
-            if n not in wide:
-                wide[n] = work.tile([LANES, PACK, COLS], BF16, name="wide", tag="wide", bufs=2)
             for t in ts:
                 for j in range(BLOCKS):
-                    cols = slice(j * LANES, (j + 1) * LANES)
-                    jj = g * BLOCKS + j
-                    nc.vector.tensor_scalar(
-                        out=wide[n][:, t, cols],
-                        in0=hr_raw[n][:, t, cols].bitcast(FP8),
-                        scalar1=sc[:, a, t, jj : jj + 1],
-                        scalar2=None,
-                        op0=ALU.mult,
-                    )
+                    if BLOCKS * t + j < PACK * BLOCKS - WIDEN_A[n] - WIDEN_B[n]:
+                        widen_block("V", n, t, j)
+
+        def widen_scalar(n, part):
+            if n >= PAIRS:
+                return
+            total = PACK * BLOCKS
+            lo, hi_ = (total - WIDEN_A[n], total) if part == 0 else (total - WIDEN_A[n] - WIDEN_B[n], total - WIDEN_A[n])
+            for k in range(lo, hi_):
+                widen_block("S", n, k // BLOCKS, k % BLOCKS)
 
         def group_tile():
             return work.tile([LANES, COLS, PACK], BF16, name="grp", tag="grp", bufs=5, align_bytes=64)
@@ -137,26 +152,33 @@ def tile_socsaerialimageacidquencherbake_d1p_kernel(
         sq = {}
         acc = {}
 
-        def multiply(codes, scales):
+        def multiply(codes, scales, bt):
+            bank = psum.tile([LANES, COLS], F32, name="mx", tag="mx", bufs=4)
+            rows = slice(bt * LANES, (bt + 1) * LANES)
+            nc.tensor.matmul_mx(
+                out=bank[:],
+                lhsT=mcodes[:, rows].bitcast(E4M3X4),
+                lhsT_scale=mscales[:, rows],
+                rhs=codes[:].bitcast(E4M3X4),
+                rhs_scale=scales[:],
+                start=True,
+                stop=True,
+            )
+            return bank
+
+        def stream(u, codes, scales, pending):
             banks = []
-            for bt in range(TILES):
-                bank = psum.tile([LANES, COLS], F32, name="mx", tag="mx", bufs=4)
-                rows = slice(bt * LANES, (bt + 1) * LANES)
-                nc.tensor.matmul_mx(
-                    out=bank[:],
-                    lhsT=mcodes[:, rows].bitcast(E4M3X4),
-                    lhsT_scale=mscales[:, rows],
-                    rhs=codes[:].bitcast(E4M3X4),
-                    rhs_scale=scales[:],
-                    start=True,
-                    stop=True,
-                )
-                banks.append(bank)
+            parts = TILES // RUN
+            for k in range(parts):
+                for bt in range(k * RUN, (k + 1) * RUN):
+                    banks.append(multiply(codes, scales, bt))
+                for x, bt in pending[k * len(pending) // parts : (k + 1) * len(pending) // parts]:
+                    turn(x, bt)
             return banks
 
         def square(u, bt, bank):
             a = (u // 2) % K
-            t = work.tile([LANES, PACK, LANES], F32, name="sq", tag="sq%d" % bt, bufs=4)
+            t = work.tile([LANES, PACK, LANES], F32, name="sq", tag="sq%d" % bt, bufs=5)
             nc.scalar.activation(
                 out=t[:], in_=bank[:].rearrange("p (q t) -> p t q", t=PACK), func=ACT.Square, scale=root[:, a : a + 1]
             )
@@ -229,6 +251,18 @@ def tile_socsaerialimageacidquencherbake_d1p_kernel(
                     in_=ngrp0[:].rearrange("p c b t -> p (c b t)"),
                 )
 
+        zero = keep.tile([LANES, COLS], BF16, name="zero")
+        nc.vector.memset(zero[:], 0.0)
+
+        def warm(count):
+            if count:
+                idle = psum.tile([LANES, COLS], F32, name="idle", tag="acc", bufs=4)
+                for k in range(count):
+                    nc.tensor.matmul(idle[:], lhsT=zero[:, 0:LANES], rhs=zero[:], start=True, stop=True)
+
+        warm(WARM[0])
+
+        widen_scalar(0, 0)
         widen(0, range(4))
         g_hr = group_tile()
         interleave(nc.vector.tensor_copy, g_hr, wide[0], 0, COLS)
@@ -246,12 +280,14 @@ def tile_socsaerialimageacidquencherbake_d1p_kernel(
                 out=dst.rearrange("p (c r u) -> p c r u", c=2, u=2),
                 in_=bank[:].rearrange("p c u r -> p c r u"),
             )
+        warm(WARM[1])
         mcodes = keep.tile([LANES, B], U32, name="mcodes", align_bytes=64)
         mscales = keep.tile([LANES, B], U8, name="mscales", align_bytes=64)
         nc.vector.quantize_mx(
             out=mcodes[:].bitcast(E4M3X4), scales=mscales[:], in_=mgrp[:].rearrange("p b t -> p (b t)")
         )
 
+        pending = []
         for n in range(PAIRS):
             u = 2 * n
             if n > 0:
@@ -259,41 +295,58 @@ def tile_socsaerialimageacidquencherbake_d1p_kernel(
                 interleave(nc.vector.tensor_copy, g_hr, wide[n], 0, COLS)
                 widen(n + 1, (0, 1))
             codes, scales = quantise(g_hr)
-            banks = multiply(codes, scales)
+            banks = stream(u, codes, scales, pending)
+            pending = [(u, bt) for bt in range(TILES) if bt not in PRE[n]]
             if n == 0:
                 hi_scalar(0)
+            widen_scalar(n + 1, 0)
             for bt in range(TILES):
                 square(u, bt, banks[bt])
             hi_scalar(n + 1)
-            if n > 0:
+            if n == K:
                 for bt in range(TILES):
-                    if bt not in PRE[n - 1]:
-                        turn(u - 1, bt)
-                if n == K:
-                    for bt in range(TILES):
-                        decay(0, bt, e0[:, bt])
-                hi_vector(n)
+                    decay(0, bt, e0[:, bt])
+            hi_vector(n)
+            if n > 0:
                 widen(n + 1, (2, 3))
                 net0_step(n)
             else:
-                hi_vector(n)
                 widen(n + 1, (0, 1))
             codes, scales = quantise(hi_grp[n])
             if n == 0:
                 widen(n + 1, (2, 3))
-            banks = multiply(codes, scales)
+            if n > 0:
+                for bt in PRE[n - 1]:
+                    preadd(n - 1, bt)
+                    pending.append((u - 1, bt))
+            banks = stream(u + 1, codes, scales, pending)
+            pending = [(u + 1, bt) for bt in range(TILES) if bt not in PRE[n]]
             if n < PAIRS - 1:
+                widen_scalar(n + 2, 1)
                 for bt in range(TILES):
                     square(u + 1, bt, banks[bt])
-                for bt in range(TILES):
-                    turn(u, bt)
 
         u = 2 * PAIRS - 1
         net0_step(PAIRS)
 
-        for bt in range(TILES):
-            turn(u - 1, bt)
+        z = {}
+
+        def bake(g, bt, ph):
+            if g == 0:
+                z[bt, ph] = psum.tile([LANES, COLS], F32, name="z", tag=("mx" if bt < 2 else "acc"), bufs=4)
+            rows = slice(bt * LANES, (bt + 1) * LANES)
+            nc.tensor.matmul_mx(
+                out=z[bt, ph][:],
+                lhsT=(ncodes0[:, rows] if g == 0 else ncode1[bt][:]).bitcast(E4M3X4),
+                lhsT_scale=(nscales0[:, rows] if g == 0 else nscale1[bt][:]),
+                rhs=bw[:, g, ph * 1024 : (ph + 1) * 1024].bitcast(E2M1X4),
+                rhs_scale=bs[:, g, ph * COLS : (ph + 1) * COLS],
+                start=(g == 0),
+                stop=(g == HALVES - 1),
+            )
+
         e1 = {}
+        ncode1, nscale1 = {}, {}
 
         def finish_decay(bt):
             e1[bt] = work.tile([LANES, PACK, LANES], F32, name="e1", tag="e1", bufs=4)
@@ -304,12 +357,13 @@ def tile_socsaerialimageacidquencherbake_d1p_kernel(
             if bt in PRE[PAIRS - 1]:
                 preadd(PAIRS - 1, bt)
             turn(u, bt)
+            bake(0, bt // 2, bt % 2)
             if bt >= 2:
                 finish_decay(bt - 2)
         finish_decay(2)
         finish_decay(3)
 
-        net1, ngrp1, ncode1, nscale1 = {}, {}, {}, {}
+        net1, ngrp1 = {}, {}
 
         def net_affine(bt):
             net1[bt] = work.tile([LANES, PACK, LANES], BF16, name="net1", tag="net1", bufs=4)
@@ -342,22 +396,6 @@ def tile_socsaerialimageacidquencherbake_d1p_kernel(
                 net_affine(bt + 1)
             net_quantise(bt)
 
-        z = {}
-
-        def bake(g, bt, ph):
-            if g == 0:
-                z[bt, ph] = psum.tile([LANES, COLS], F32, name="z", tag=("mx" if bt < 2 else "acc"), bufs=4)
-            rows = slice(bt * LANES, (bt + 1) * LANES)
-            nc.tensor.matmul_mx(
-                out=z[bt, ph][:],
-                lhsT=(ncodes0[:, rows] if g == 0 else ncode1[bt][:]).bitcast(E4M3X4),
-                lhsT_scale=(nscales0[:, rows] if g == 0 else nscale1[bt][:]),
-                rhs=bw[:, g, ph * 1024 : (ph + 1) * 1024].bitcast(E2M1X4),
-                rhs_scale=bs[:, g, ph * COLS : (ph + 1) * COLS],
-                start=(g == 0),
-                stop=(g == HALVES - 1),
-            )
-
         def finish(bt, ph):
             rows = slice(bt * LANES, (bt + 1) * LANES)
             th = work.tile([LANES, COLS], F32, name="th", tag="th", bufs=4)
@@ -367,9 +405,10 @@ def tile_socsaerialimageacidquencherbake_d1p_kernel(
             nc.sync.dma_start(out=out[rows, ph * COLS : (ph + 1) * COLS], in_=o[:])
 
         for h in range(2):
-            for bt in (2 * h, 2 * h + 1):
-                for ph in range(2):
-                    bake(0, bt, ph)
+            if h == 1:
+                for bt in (2, 3):
+                    for ph in range(2):
+                        bake(0, bt, ph)
             for bt in (2 * h, 2 * h + 1):
                 for ph in range(2):
                     bake(1, bt, ph)

@@ -24,12 +24,13 @@ TILES = B // LANES
 HALVES = M // COLS
 BLOCKS = COLS // LANES
 PAIRS = HALVES * K
-SCALAR_COLS = (256, 0, 0, 0, 0, 0, 0, 0)
-PRE = ((), (), (), (), (), (), (), (0, 1, 2, 3,))
-NET0 = (8, 8, 8)
+SCALAR_COLS = (256, 64, 0, 0, 0, 0, 0, 0)
+PRE = ((), (), (), (), (), (), (0,), (0, 1, 2,))
+NET0 = (5, 6, 7)
 RUN = 4
 WARM = (6, 6)
-WIDEN_A = (5, 0, 0, 0, 0, 0, 0, 0)
+WSPLIT = 4
+WIDEN_A = (6, 6, 3, 3, 4, 3, 2, 3)
 WIDEN_B = (0, 0, 0, 0, 0, 0, 0, 0)
 
 
@@ -42,6 +43,9 @@ def tile_socsaerialimageacidquencherbake_d1p_kernel(
         work = ctx.enter_context(tc.tile_pool(name="work", bufs=3))
         psum = ctx.enter_context(tc.psum_pool(name="psum", bufs=4))
         ctx.enter_context(tc.manual_schedule())
+
+        zero = keep.tile([LANES, COLS], BF16, name="zero")
+        nc.vector.memset(zero[:], 0.0)
 
         sc = keep.tile([LANES, K, PACK, M // LANES], F32, name="sc")
         nc.sync.dma_start(out=sc[:], in_=hr_scale.rearrange("a (p t) j -> p a t j", t=PACK))
@@ -84,7 +88,7 @@ def tile_socsaerialimageacidquencherbake_d1p_kernel(
         bw = keep.tile([LANES, HALVES, 2 * P], U8, name="bw", align_bytes=64)
         nc.sync.dma_start(out=bw[:].bitcast(I32), in_=bake_words.bitcast(I32).rearrange("g p w -> p g w"))
         bs = keep.tile([LANES, HALVES, P], U8, name="bs", align_bytes=64)
-        nc.gpsimd.memset(bs[:].bitcast(I32), 0)
+        nc.vector.memset(bs[:].bitcast(I32), 0)
         for q in range(4):
             nc.sync.dma_start(
                 out=bs[32 * q : 32 * q + 4].bitcast(I32),
@@ -98,9 +102,7 @@ def tile_socsaerialimageacidquencherbake_d1p_kernel(
         root = keep.tile([LANES, K], F32, name="root")
         nc.gpsimd.tensor_tensor(out=root[:], in0=om[:], in1=half[:], op=ALU.pow)
         nrho = keep.tile([LANES, HALVES, PACK], F32, name="nrho")
-        nc.gpsimd.tensor_scalar(out=nrho[:], in0=rh[:], scalar1=-1.0, scalar2=0.0, op0=ALU.mult, op1=ALU.add)
         omq = keep.tile([LANES, HALVES, PACK], F32, name="omq")
-        nc.gpsimd.tensor_scalar(out=omq[:], in0=qu[:], scalar1=-1.0, scalar2=1.0, op0=ALU.mult, op1=ALU.add)
 
         wide = {}
 
@@ -117,13 +119,13 @@ def tile_socsaerialimageacidquencherbake_d1p_kernel(
             else:
                 nc.vector.tensor_scalar(out=dst, in0=src, scalar1=scale, scalar2=None, op0=ALU.mult)
 
-        def widen(n, ts):
+        def widen(n, part):
             if n >= PAIRS:
                 return
-            for t in ts:
-                for j in range(BLOCKS):
-                    if BLOCKS * t + j < PACK * BLOCKS - WIDEN_A[n] - WIDEN_B[n]:
-                        widen_block("V", n, t, j)
+            mine = PACK * BLOCKS - WIDEN_A[n] - WIDEN_B[n]
+            cut = mine if part is None else min(mine, WSPLIT)
+            for k in range(0 if part in (None, 0) else cut, cut if part in (None, 0) else mine):
+                widen_block("V", n, k // BLOCKS, k % BLOCKS)
 
         def widen_scalar(n, part):
             if n >= PAIRS:
@@ -251,9 +253,6 @@ def tile_socsaerialimageacidquencherbake_d1p_kernel(
                     in_=ngrp0[:].rearrange("p c b t -> p (c b t)"),
                 )
 
-        zero = keep.tile([LANES, COLS], BF16, name="zero")
-        nc.vector.memset(zero[:], 0.0)
-
         def warm(count):
             if count:
                 idle = psum.tile([LANES, COLS], F32, name="idle", tag="acc", bufs=4)
@@ -263,7 +262,7 @@ def tile_socsaerialimageacidquencherbake_d1p_kernel(
         warm(WARM[0])
 
         widen_scalar(0, 0)
-        widen(0, range(4))
+        widen(0, None)
         g_hr = group_tile()
         interleave(nc.vector.tensor_copy, g_hr, wide[0], 0, COLS)
 
@@ -293,7 +292,7 @@ def tile_socsaerialimageacidquencherbake_d1p_kernel(
             if n > 0:
                 g_hr = group_tile()
                 interleave(nc.vector.tensor_copy, g_hr, wide[n], 0, COLS)
-                widen(n + 1, (0, 1))
+                widen(n + 1, 0)
             codes, scales = quantise(g_hr)
             banks = stream(u, codes, scales, pending)
             pending = [(u, bt) for bt in range(TILES) if bt not in PRE[n]]
@@ -308,13 +307,16 @@ def tile_socsaerialimageacidquencherbake_d1p_kernel(
                     decay(0, bt, e0[:, bt])
             hi_vector(n)
             if n > 0:
-                widen(n + 1, (2, 3))
+                widen(n + 1, 1)
                 net0_step(n)
             else:
-                widen(n + 1, (0, 1))
+                widen(n + 1, 0)
             codes, scales = quantise(hi_grp[n])
             if n == 0:
-                widen(n + 1, (2, 3))
+                widen(n + 1, 1)
+            if n == 2:
+                nc.vector.tensor_scalar(out=nrho[:], in0=rh[:], scalar1=-1.0, scalar2=None, op0=ALU.mult)
+                nc.vector.tensor_scalar(out=omq[:], in0=qu[:], scalar1=-1.0, scalar2=1.0, op0=ALU.mult, op1=ALU.add)
             if n > 0:
                 for bt in PRE[n - 1]:
                     preadd(n - 1, bt)
@@ -398,11 +400,17 @@ def tile_socsaerialimageacidquencherbake_d1p_kernel(
 
         def finish(bt, ph):
             rows = slice(bt * LANES, (bt + 1) * LANES)
+            pieces = 2 if (bt, ph) == (TILES - 1, 1) else 1
+            width = COLS // pieces
             th = work.tile([LANES, COLS], F32, name="th", tag="th", bufs=4)
-            nc.scalar.activation(out=th[:], in_=z[bt, ph][:], func=ACT.Tanh, scale=0.5)
             o = work.tile([LANES, COLS], F32, name="o", tag="o", bufs=8)
-            nc.vector.tensor_scalar(out=o[:], in0=th[:], scalar1=0.5, scalar2=0.5, op0=ALU.mult, op1=ALU.add)
-            nc.sync.dma_start(out=out[rows, ph * COLS : (ph + 1) * COLS], in_=o[:])
+            for k in range(pieces):
+                cols = slice(k * width, (k + 1) * width)
+                nc.scalar.activation(out=th[:, cols], in_=z[bt, ph][:, cols], func=ACT.Tanh, scale=0.5)
+                nc.vector.tensor_scalar(
+                    out=o[:, cols], in0=th[:, cols], scalar1=0.5, scalar2=0.5, op0=ALU.mult, op1=ALU.add
+                )
+                nc.sync.dma_start(out=out[rows, ph * COLS + k * width : ph * COLS + (k + 1) * width], in_=o[:, cols])
 
         for h in range(2):
             if h == 1:

@@ -24,13 +24,13 @@ TILES = B // LANES
 HALVES = M // COLS
 BLOCKS = COLS // LANES
 PAIRS = HALVES * K
-SCALAR_COLS = (256, 64, 0, 0, 0, 0, 0, 0)
-PRE = ((), (), (), (), (), (), (0,), (0, 1, 2,))
+SCALAR_COLS = (256, 0, 0, 0, 0, 0, 0, 0)
+PRE = ((), (), (), (), (), (), (0, 1,), (0, 1, 2,))
 NET0 = (5, 6, 7)
 RUN = 4
 WARM = (6, 6)
-WSPLIT = 4
-WIDEN_A = (6, 6, 3, 3, 4, 3, 2, 3)
+WSPLIT = 12
+WIDEN_A = (6, 6, 3, 3, 3, 3, 3, 3)
 WIDEN_B = (0, 0, 0, 0, 0, 0, 0, 0)
 
 
@@ -48,7 +48,7 @@ def tile_socsaerialimageacidquencherbake_d1p_kernel(
         nc.vector.memset(zero[:], 0.0)
 
         sc = keep.tile([LANES, K, PACK, M // LANES], F32, name="sc")
-        nc.sync.dma_start(out=sc[:], in_=hr_scale.rearrange("a (p t) j -> p a t j", t=PACK))
+        nc.scalar.dma_start(out=sc[:], in_=hr_scale.rearrange("a (p t) j -> p a t j", t=PACK))
         om = keep.tile([LANES, K], BF16, name="om")
         nc.scalar.dma_start(out=om[:], in_=omega.partition_broadcast(LANES))
 

from contextlib import ExitStack

import concourse.mybir as mybir
from concourse.masks import make_identity

B, N, K, M, P = 512, 512, 4, 1024, 1024
FLOPS = 2 * (B * N * M * K * 2 + B * M * P)

F32 = mybir.dt.float32
BF16 = mybir.dt.bfloat16
U8 = mybir.dt.uint8
U32 = mybir.dt.uint32
I32 = mybir.dt.int32
FP8 = mybir.dt.float8_e4m3fn
E4M3X4 = mybir.dt.float8_e4m3fn_x4
E2M1X4 = mybir.dt.float4_e2m1fn_x4
ALU = mybir.AluOpType
ACT = mybir.ActivationFunctionType

LANES = 128
PACK = 4
COLS = 512
TILES = B // LANES
HALVES = M // COLS
BLOCKS = COLS // LANES
PAIRS = HALVES * K
SCALAR_COLS = (256, 0, 0, 0, 0, 0, 0, 0)
PRE = ((), (), (), (), (), (), (0, 1,), (0, 1, 2,))
NET0 = (5, 6, 7)
RUN = 4
WARM = (6, 6)
WSPLIT = 12
WIDEN_A = (6, 6, 3, 3, 3, 3, 3, 3)
WIDEN_B = (0, 0, 0, 0, 0, 0, 0, 0)


def tile_socsaerialimageacidquencherbake_d1p_kernel(
    tc, mask, hr_bytes, hr_scale, hi, omega, quench, rho, bake_words, bake_scales, out
):
    nc = tc.nc
    with ExitStack() as ctx:
        keep = ctx.enter_context(tc.tile_pool(name="keep", bufs=1))
        work = ctx.enter_context(tc.tile_pool(name="work", bufs=3))
        psum = ctx.enter_context(tc.psum_pool(name="psum", bufs=4))
        ctx.enter_context(tc.manual_schedule())

        zero = keep.tile([LANES, COLS], BF16, name="zero")
        nc.vector.memset(zero[:], 0.0)

        sc = keep.tile([LANES, K, PACK, M // LANES], F32, name="sc")
        nc.scalar.dma_start(out=sc[:], in_=hr_scale.rearrange("a (p t) j -> p a t j", t=PACK))
        om = keep.tile([LANES, K], BF16, name="om")
        nc.scalar.dma_start(out=om[:], in_=omega.partition_broadcast(LANES))

        hr_raw, hi_raw = {}, {}

        def load_hr(n):
            g, a = divmod(n, K)
            t = keep.tile([LANES, PACK, COLS], U8, name="hrb%d" % n)
            nc.sync.dma_start(
                out=t[:],
                in_=hr_bytes[a].rearrange("(p t) m -> p t m", t=PACK)[:, :, g * COLS : (g + 1) * COLS],
            )
            hr_raw[n] = t

        def load_hi(n):
            g, a = divmod(n, K)
            t = keep.tile([LANES, PACK, COLS], BF16, name="hib%d" % n)
            nc.sync.dma_start(
                out=t[:],
                in_=hi[a].rearrange("(p t) m -> p t m", t=PACK)[:, :, g * COLS : (g + 1) * COLS],
            )
            hi_raw[n] = t

        load_hr(0)
        mraw = keep.tile([LANES, TILES, N], BF16, name="mraw")
        mview = mask.rearrange("(c p) n -> p c n", p=LANES)
        nc.sync.dma_start(out=mraw[:, 0:2, :], in_=mview[:, 0:2, :])
        nc.sync.dma_start(out=mraw[:, 2:4, :], in_=mview[:, 2:4, :])
        load_hi(0)
        rh = keep.tile([LANES, HALVES, PACK], BF16, name="rh")
        nc.scalar.dma_start(out=rh[:], in_=rho.rearrange("(g p t) -> p g t", p=LANES, t=PACK))
        qu = keep.tile([LANES, HALVES, PACK], BF16, name="qu")
        nc.scalar.dma_start(out=qu[:], in_=quench.rearrange("(g p t) -> p g t", p=LANES, t=PACK))
        for n in range(1, PAIRS):
            load_hr(n)
            load_hi(n)
        bw = keep.tile([LANES, HALVES, 2 * P], U8, name="bw", align_bytes=64)
        nc.sync.dma_start(out=bw[:].bitcast(I32), in_=bake_words.bitcast(I32).rearrange("g p w -> p g w"))
        bs = keep.tile([LANES, HALVES, P], U8, name="bs", align_bytes=64)
        nc.vector.memset(bs[:].bitcast(I32), 0)
        for q in range(4):
            nc.sync.dma_start(
                out=bs[32 * q : 32 * q + 4].bitcast(I32),
                in_=bake_scales[:, 4 * q : 4 * q + 4, :].bitcast(I32).rearrange("g q w -> q g w"),
            )

        ident = keep.tile([LANES, LANES], F32, name="ident")
        make_identity(nc, ident[:])
        half = keep.tile([LANES, K], F32, name="half")
        nc.gpsimd.memset(half[:], 0.5)
        root = keep.tile([LANES, K], F32, name="root")
        nc.gpsimd.tensor_tensor(out=root[:], in0=om[:], in1=half[:], op=ALU.pow)
        nrho = keep.tile([LANES, HALVES, PACK], F32, name="nrho")
        omq = keep.tile([LANES, HALVES, PACK], F32, name="omq")

        wide = {}

        def widen_block(engine, n, t, j):
            g, a = divmod(n, K)
            if n not in wide:
                wide[n] = work.tile([LANES, PACK, COLS], BF16, name="wide", tag="wide", bufs=3)
            cols = slice(j * LANES, (j + 1) * LANES)
            scale = sc[:, a, t, g * BLOCKS + j : g * BLOCKS + j + 1]
            dst = wide[n][:, t, cols]
            src = hr_raw[n][:, t, cols].bitcast(FP8)
            if engine == "S":
                nc.scalar.activation(out=dst, in_=src, func=ACT.Copy, scale=scale)
            else:
                nc.vector.tensor_scalar(out=dst, in0=src, scalar1=scale, scalar2=None, op0=ALU.mult)

        def widen(n, part):
            if n >= PAIRS:
                return
            mine = PACK * BLOCKS - WIDEN_A[n] - WIDEN_B[n]
            cut = mine if part is None else min(mine, WSPLIT)
            for k in range(0 if part in (None, 0) else cut, cut if part in (None, 0) else mine):
                widen_block("V", n, k // BLOCKS, k % BLOCKS)

        def widen_scalar(n, part):
            if n >= PAIRS:
                return
            total = PACK * BLOCKS
            lo, hi_ = (total - WIDEN_A[n], total) if part == 0 else (total - WIDEN_A[n] - WIDEN_B[n], total - WIDEN_A[n])
            for k in range(lo, hi_):
                widen_block("S", n, k // BLOCKS, k % BLOCKS)

        def group_tile():
            return work.tile([LANES, COLS, PACK], BF16, name="grp", tag="grp", bufs=5, align_bytes=64)

        def interleave(engine_copy, dst, src4, c0, c1):
            d = dst[:, c0:c1, :].rearrange("p (c i) t -> p c t i", i=4)
            s = src4[:, :, c0:c1].rearrange("p t (c i) -> p c t i", i=4)
            engine_copy(out=d, in_=s)

        def quantise(grp):
            codes = work.tile([LANES, COLS], U32, name="codes", tag="codes", bufs=4, align_bytes=64)
            scales = work.tile([LANES, COLS], U8, name="scales", tag="scales", bufs=4, align_bytes=64)
            nc.vector.quantize_mx(
                out=codes[:].bitcast(E4M3X4), scales=scales[:], in_=grp[:].rearrange("p c t -> p (c t)")
            )
            return codes, scales

        sq = {}
        acc = {}

        def multiply(codes, scales, bt):
            bank = psum.tile([LANES, COLS], F32, name="mx", tag="mx", bufs=4)
            rows = slice(bt * LANES, (bt + 1) * LANES)
            nc.tensor.matmul_mx(
                out=bank[:],
                lhsT=mcodes[:, rows].bitcast(E4M3X4),
                lhsT_scale=mscales[:, rows],
                rhs=codes[:].bitcast(E4M3X4),
                rhs_scale=scales[:],
                start=True,
                stop=True,
            )
            return bank

        def stream(u, codes, scales, pending):
            banks = []
            parts = TILES // RUN
            for k in range(parts):
                for bt in range(k * RUN, (k + 1) * RUN):
                    banks.append(multiply(codes, scales, bt))
                for x, bt in pending[k * len(pending) // parts : (k + 1) * len(pending) // parts]:
                    turn(x, bt)
            return banks

        def square(u, bt, bank):
            a = (u // 2) % K
            t = work.tile([LANES, PACK, LANES], F32, name="sq", tag="sq%d" % bt, bufs=5)
            nc.scalar.activation(
                out=t[:], in_=bank[:].rearrange("p (q t) -> p t q", t=PACK), func=ACT.Square, scale=root[:, a : a + 1]
            )
            sq[u, bt] = t

        def preadd(n, bt):
            s = work.tile([LANES, PACK, LANES], F32, name="sum", tag="sum", bufs=4)
            nc.vector.tensor_tensor(out=s[:], in0=sq[2 * n, bt][:], in1=sq[2 * n + 1, bt][:], op=ALU.add)
            sq[2 * n + 1, bt] = s

        def turn(u, bt):
            n, odd = divmod(u, 2)
            g, a = divmod(n, K)
            if not odd and bt in PRE[n]:
                return
            first = (g, bt) not in acc
            if first:
                acc[g, bt] = psum.tile([LANES, PACK, LANES], F32, name="acc", tag="acc", bufs=4)
            final = odd and a == K - 1
            for t in range(PACK):
                nc.tensor.matmul(
                    acc[g, bt][:, t, :],
                    lhsT=sq[u, bt][:, t, :],
                    rhs=ident[:],
                    is_transpose=True,
                    start=bool(first and t == 0),
                    stop=bool(final and t == PACK - 1),
                )

        def decay(g, bt, dst):
            nc.scalar.activation(out=dst, in_=acc[g, bt][:], func=ACT.Exp, scale=-1.0)

        e0 = keep.tile([LANES, TILES, PACK, LANES], F32, name="e0")
        net0 = keep.tile([LANES, TILES, PACK, LANES], BF16, name="net0")
        ngrp0 = keep.tile([LANES, TILES, LANES, PACK], BF16, name="ngrp0", align_bytes=64)
        ncodes0 = keep.tile([LANES, B], U32, name="ncodes0", align_bytes=64)
        nscales0 = keep.tile([LANES, B], U8, name="nscales0", align_bytes=64)

        hi_grp = {}

        def hi_vector(n):
            cut = SCALAR_COLS[n]
            if n not in hi_grp:
                hi_grp[n] = group_tile()
            if cut < COLS:
                interleave(nc.vector.tensor_copy, hi_grp[n], hi_raw[n], cut, COLS)

        def hi_scalar(n):
            if n < PAIRS and SCALAR_COLS[n]:
                hi_grp[n] = group_tile()
                interleave(nc.scalar.copy, hi_grp[n], hi_raw[n], 0, SCALAR_COLS[n])

        def net0_step(n):
            if n == NET0[0]:
                for t in range(PACK):
                    nc.vector.tensor_scalar(
                        out=net0[:, :, t, :],
                        in0=e0[:, :, t, :],
                        scalar1=omq[:, 0, t : t + 1],
                        scalar2=nrho[:, 0, t : t + 1],
                        op0=ALU.subtract,
                        op1=ALU.mult,
                    )
            if n == NET0[1]:
                nc.vector.tensor_copy(out=ngrp0[:], in_=net0[:].rearrange("p c t b -> p c b t"))
            if n == NET0[2]:
                nc.vector.quantize_mx(
                    out=ncodes0[:].bitcast(E4M3X4),
                    scales=nscales0[:],
                    in_=ngrp0[:].rearrange("p c b t -> p (c b t)"),
                )

        def warm(count):
            if count:
                idle = psum.tile([LANES, COLS], F32, name="idle", tag="acc", bufs=4)
                for k in range(count):
                    nc.tensor.matmul(idle[:], lhsT=zero[:, 0:LANES], rhs=zero[:], start=True, stop=True)

        warm(WARM[0])

        widen_scalar(0, 0)
        widen(0, None)
        g_hr = group_tile()
        interleave(nc.vector.tensor_copy, g_hr, wide[0], 0, COLS)

        mgrp = keep.tile([LANES, B, PACK], BF16, name="mgrp", align_bytes=64)
        mwords = mraw[:].rearrange("p c n -> p (c n)").bitcast(F32)
        for h in range(2):
            bank = psum.tile([LANES, 2, 2, LANES], F32, name="mx", tag="mx", bufs=4)
            for c in range(2):
                for u in range(2):
                    base = (2 * h + c) * (N // 2)
                    nc.tensor.transpose(bank[:, c, u, :], mwords[:, base + u : base + N // 2 : 2], ident[:])
            dst = mgrp[:, h * 256 : (h + 1) * 256, :].rearrange("p b t -> p (b t)").bitcast(F32)
            nc.scalar.copy(
                out=dst.rearrange("p (c r u) -> p c r u", c=2, u=2),
                in_=bank[:].rearrange("p c u r -> p c r u"),
            )
        warm(WARM[1])
        mcodes = keep.tile([LANES, B], U32, name="mcodes", align_bytes=64)
        mscales = keep.tile([LANES, B], U8, name="mscales", align_bytes=64)
        nc.vector.quantize_mx(
            out=mcodes[:].bitcast(E4M3X4), scales=mscales[:], in_=mgrp[:].rearrange("p b t -> p (b t)")
        )

        pending = []
        for n in range(PAIRS):
            u = 2 * n
            if n > 0:
                g_hr = group_tile()
                interleave(nc.vector.tensor_copy, g_hr, wide[n], 0, COLS)
                widen(n + 1, 0)
            codes, scales = quantise(g_hr)
            banks = stream(u, codes, scales, pending)
            pending = [(u, bt) for bt in range(TILES) if bt not in PRE[n]]
            if n == 0:
                hi_scalar(0)
            widen_scalar(n + 1, 0)
            for bt in range(TILES):
                square(u, bt, banks[bt])
            hi_scalar(n + 1)
            if n == K:
                for bt in range(TILES):
                    decay(0, bt, e0[:, bt])
            hi_vector(n)
            if n > 0:
                widen(n + 1, 1)
                net0_step(n)
            else:
                widen(n + 1, 0)
            codes, scales = quantise(hi_grp[n])
            if n == 0:
                widen(n + 1, 1)
            if n == 2:
                nc.vector.tensor_scalar(out=nrho[:], in0=rh[:], scalar1=-1.0, scalar2=None, op0=ALU.mult)
                nc.vector.tensor_scalar(out=omq[:], in0=qu[:], scalar1=-1.0, scalar2=1.0, op0=ALU.mult, op1=ALU.add)
            if n > 0:
                for bt in PRE[n - 1]:
                    preadd(n - 1, bt)
                    pending.append((u - 1, bt))
            banks = stream(u + 1, codes, scales, pending)
            pending = [(u + 1, bt) for bt in range(TILES) if bt not in PRE[n]]
            if n < PAIRS - 1:
                widen_scalar(n + 2, 1)
                for bt in range(TILES):
                    square(u + 1, bt, banks[bt])

        u = 2 * PAIRS - 1
        net0_step(PAIRS)

        z = {}

        def bake(g, bt, ph):
            if g == 0:
                z[bt, ph] = psum.tile([LANES, COLS], F32, name="z", tag=("mx" if bt < 2 else "acc"), bufs=4)
            rows = slice(bt * LANES, (bt + 1) * LANES)
            nc.tensor.matmul_mx(
                out=z[bt, ph][:],
                lhsT=(ncodes0[:, rows] if g == 0 else ncode1[bt][:]).bitcast(E4M3X4),
                lhsT_scale=(nscales0[:, rows] if g == 0 else nscale1[bt][:]),
                rhs=bw[:, g, ph * 1024 : (ph + 1) * 1024].bitcast(E2M1X4),
                rhs_scale=bs[:, g, ph * COLS : (ph + 1) * COLS],
                start=(g == 0),
                stop=(g == HALVES - 1),
            )

        e1 = {}
        ncode1, nscale1 = {}, {}

        def finish_decay(bt):
            e1[bt] = work.tile([LANES, PACK, LANES], F32, name="e1", tag="e1", bufs=4)
            decay(1, bt, e1[bt][:])

        for bt in range(TILES):
            square(u, bt, banks[bt])
            if bt in PRE[PAIRS - 1]:
                preadd(PAIRS - 1, bt)
            turn(u, bt)
            bake(0, bt // 2, bt % 2)
            if bt >= 2:
                finish_decay(bt - 2)
        finish_decay(2)
        finish_decay(3)

        net1, ngrp1 = {}, {}

        def net_affine(bt):
            net1[bt] = work.tile([LANES, PACK, LANES], BF16, name="net1", tag="net1", bufs=4)
            for t in range(PACK):
                nc.vector.tensor_scalar(
                    out=net1[bt][:, t, :],
                    in0=e1[bt][:, t, :],
                    scalar1=omq[:, 1, t : t + 1],
                    scalar2=nrho[:, 1, t : t + 1],
                    op0=ALU.subtract,
                    op1=ALU.mult,
                )

        def net_group(bt):
            ngrp1[bt] = work.tile([LANES, LANES, PACK], BF16, name="ngrp1", tag="ngrp1", bufs=4, align_bytes=64)
            interleave(nc.vector.tensor_copy, ngrp1[bt], net1[bt], 0, LANES)

        def net_quantise(bt):
            c1 = work.tile([LANES, LANES], U32, name="nc1", tag="nc1", bufs=4, align_bytes=64)
            s1 = work.tile([LANES, LANES], U8, name="ns1", tag="ns1", bufs=4, align_bytes=64)
            nc.vector.quantize_mx(
                out=c1[:].bitcast(E4M3X4), scales=s1[:], in_=ngrp1[bt][:].rearrange("p b t -> p (b t)")
            )
            ncode1[bt], nscale1[bt] = c1, s1

        net_affine(0)
        for bt in range(TILES):
            net_group(bt)
            if bt + 1 < TILES:
                net_affine(bt + 1)
            net_quantise(bt)

        def finish(bt, ph):
            rows = slice(bt * LANES, (bt + 1) * LANES)
            pieces = 2 if (bt, ph) == (TILES - 1, 1) else 1
            width = COLS // pieces
            th = work.tile([LANES, COLS], F32, name="th", tag="th", bufs=4)
            o = work.tile([LANES, COLS], F32, name="o", tag="o", bufs=8)
            for k in range(pieces):
                cols = slice(k * width, (k + 1) * width)
                nc.scalar.activation(out=th[:, cols], in_=z[bt, ph][:, cols], func=ACT.Tanh, scale=0.5)
                nc.vector.tensor_scalar(
                    out=o[:, cols], in0=th[:, cols], scalar1=0.5, scalar2=0.5, op0=ALU.mult, op1=ALU.add
                )
                nc.sync.dma_start(out=out[rows, ph * COLS + k * width : ph * COLS + (k + 1) * width], in_=o[:, cols])

        for h in range(2):
            if h == 1:
                for bt in (2, 3):
                    for ph in range(2):
                        bake(0, bt, ph)
            for bt in (2 * h, 2 * h + 1):
                for ph in range(2):
                    bake(1, bt, ph)
                    finish(bt, ph)
